import numpy as np
import ml_dtypes

BF16 = ml_dtypes.bfloat16


def bf(x):
    return np.asarray(x, np.float32).astype(BF16)


def f32(x):
    return np.asarray(x, np.float32)


def f64(x):
    return np.asarray(x).astype(np.float64)


def striped(idx):
    return np.tile(idx.reshape(-1, 16).T, (8, 1))


def rows(idx, k):
    return np.tile(idx, (k, 1))


def look(tab, idx):
    return np.take_along_axis(f64(tab), rows(idx, len(tab)), axis=1)


K, S, D, V, N, M = 128, 256, 3, 64, 192, 512


def setup_inputs():
    return {"tab": f32(np.random.standard_normal((K, S))), "x0": f32(np.random.standard_normal((K, V))), "w": bf(np.random.standard_normal((K, M)) / np.sqrt(K)), "offs": striped(np.random.permutation(S)[:N])}


def reference(tab, x0, w, offs):
    idx = offs[:16].T.reshape(-1)
    x = f64(x0)
    for d in range(D):
        x = np.minimum(x, look(tab, idx[d * V:(d + 1) * V]))
    y = f64(w).T @ x
    return y

@@ -1,0 +1,55 @@
+import concourse.mybir as mybir
+
+BF16, F32, U16 = mybir.dt.bfloat16, mybir.dt.float32, mybir.dt.uint16
+MIN = mybir.AluOpType.min
+
+P = 128
+S = 256
+D = 3
+V = 64
+M = 512
+BLOCKS = M // P
+HALF = BLOCKS // 2
+LIST_COLUMNS = V // 16
+
+FLOPS = 2 * P * M * V + D * P * V
+
+
+def tile_lookup_pool_min_none_kernel(tc, tab, x0, w, offs, out):
+    nc = tc.nc
+    with (
+        tc.tile_pool(name="held", bufs=1) as held,
+        tc.psum_pool(name="psum", bufs=1) as psum,
+    ):
+        offsets = held.tile([P, D * LIST_COLUMNS], U16)
+        nc.sync.dma_start(offsets[:], offs)
+        table = held.tile([P, S], F32)
+        nc.scalar.dma_start(table[:], tab)
+        centre = held.tile([P, V], F32)
+        nc.sync.dma_start(centre[:], x0)
+        weights = held.tile([P, M], BF16)
+        nc.scalar.dma_start(weights[:], w)
+
+        smallest = centre
+        for d in range(D):
+            neighbour = table[:].indirect(offsets[:, d * LIST_COLUMNS : (d + 1) * LIST_COLUMNS])
+            lower = held.tile([P, V], F32, name=f"lower{d}")
+            nc.vector.tensor_tensor(lower[:], neighbour, smallest[:], MIN)
+            smallest = lower
+        x = held.tile([P, V], BF16)
+        nc.vector.tensor_copy(x[:], smallest[:])
+
+        out_blocks = out.rearrange("(b p) j -> p b j", p=P)
+        for half in range(2):
+            product = psum.tile([P, HALF, V], F32, name=f"product{half}")
+            for b in range(HALF):
+                block = half * HALF + b
+                nc.tensor.matmul(product[:, b, :], weights[:, block * P : (block + 1) * P], x[:], start=True, stop=True)
+            staged = held.tile([P, HALF, V], F32, name=f"staged{half}")
+            rows = out_blocks[:, half * HALF : (half + 1) * HALF, :]
+            if half == 0:
+                nc.vector.tensor_copy(staged[:], product[:])
+                nc.sync.dma_start(rows, staged[:])
+            else:
+                nc.scalar.copy(staged[:], product[:])
+                nc.scalar.dma_start(rows, staged[:])

@@ -39,14 +39,15 @@ def tile_lookup_pool_min_none_kernel(tc, tab, x0, w, offs, out):
         x = held.tile([P, V], BF16)
         nc.vector.tensor_copy(x[:], smallest[:])
 
-        out_blocks = out.rearrange("(b p) j -> p b j", p=P)
+        out_rows = out.rearrange("(p b) j -> p b j", b=BLOCKS)
+        weight_columns = weights[:].rearrange("k (p b) -> k b p", b=BLOCKS)
         for half in range(2):
             product = psum.tile([P, HALF, V], F32, name=f"product{half}")
             for b in range(HALF):
                 block = half * HALF + b
-                nc.tensor.matmul(product[:, b, :], weights[:, block * P : (block + 1) * P], x[:], start=True, stop=True)
+                nc.tensor.matmul(product[:, b, :], weight_columns[:, block, :], x[:], start=True, stop=True)
             staged = held.tile([P, HALF, V], F32, name=f"staged{half}")
-            rows = out_blocks[:, half * HALF : (half + 1) * HALF, :]
+            rows = out_rows[:, half * HALF : (half + 1) * HALF, :]
             if half == 0:
                 nc.vector.tensor_copy(staged[:], product[:])
                 nc.sync.dma_start(rows, staged[:])

@@ -30,14 +30,14 @@ def tile_lookup_pool_min_none_kernel(tc, tab, x0, w, offs, out):
         weights = held.tile([P, M], BF16)
         nc.scalar.dma_start(weights[:], w)
 
-        smallest = centre
+        running = [centre, centre]
         for d in range(D):
             neighbour = table[:].indirect(offsets[:, d * LIST_COLUMNS : (d + 1) * LIST_COLUMNS])
             lower = held.tile([P, V], F32, name=f"lower{d}")
-            nc.vector.tensor_tensor(lower[:], neighbour, smallest[:], MIN)
-            smallest = lower
+            nc.vector.tensor_tensor(lower[:], neighbour, running[d % 2][:], MIN)
+            running[d % 2] = lower
         x = held.tile([P, V], BF16)
-        nc.vector.tensor_copy(x[:], smallest[:])
+        nc.vector.tensor_tensor(x[:], running[0][:], running[1][:], MIN)
 
         out_rows = out.rearrange("(p b) j -> p b j", b=BLOCKS)
         weight_columns = weights[:].rearrange("k (p b) -> k b p", b=BLOCKS)

@@ -41,16 +41,15 @@ def tile_lookup_pool_min_none_kernel(tc, tab, x0, w, offs, out):
 
         out_rows = out.rearrange("(p b) j -> p b j", b=BLOCKS)
         weight_columns = weights[:].rearrange("k (p b) -> k b p", b=BLOCKS)
+        staged = held.tile([P, BLOCKS, V], F32)
         for half in range(2):
             product = psum.tile([P, HALF, V], F32, name=f"product{half}")
             for b in range(HALF):
                 block = half * HALF + b
                 nc.tensor.matmul(product[:, b, :], weight_columns[:, block, :], x[:], start=True, stop=True)
-            staged = held.tile([P, HALF, V], F32, name=f"staged{half}")
-            rows = out_rows[:, half * HALF : (half + 1) * HALF, :]
+            staged_half = staged[:, half * HALF : (half + 1) * HALF, :]
             if half == 0:
-                nc.vector.tensor_copy(staged[:], product[:])
-                nc.sync.dma_start(rows, staged[:])
+                nc.vector.tensor_copy(staged_half, product[:])
             else:
-                nc.scalar.copy(staged[:], product[:])
-                nc.scalar.dma_start(rows, staged[:])
+                nc.scalar.copy(staged_half, product[:])
+        nc.sync.dma_start(out_rows, staged[:])

import concourse.mybir as mybir

BF16, F32, U16 = mybir.dt.bfloat16, mybir.dt.float32, mybir.dt.uint16
MIN = mybir.AluOpType.min

P = 128
S = 256
D = 3
V = 64
M = 512
BLOCKS = M // P
HALF = BLOCKS // 2
LIST_COLUMNS = V // 16

FLOPS = 2 * P * M * V + D * P * V


def tile_lookup_pool_min_none_kernel(tc, tab, x0, w, offs, out):
    nc = tc.nc
    with (
        tc.tile_pool(name="held", bufs=1) as held,
        tc.psum_pool(name="psum", bufs=1) as psum,
    ):
        offsets = held.tile([P, D * LIST_COLUMNS], U16)
        nc.sync.dma_start(offsets[:], offs)
        table = held.tile([P, S], F32)
        nc.scalar.dma_start(table[:], tab)
        centre = held.tile([P, V], F32)
        nc.sync.dma_start(centre[:], x0)
        weights = held.tile([P, M], BF16)
        nc.scalar.dma_start(weights[:], w)

        running = [centre, centre]
        for d in range(D):
            neighbour = table[:].indirect(offsets[:, d * LIST_COLUMNS : (d + 1) * LIST_COLUMNS])
            lower = held.tile([P, V], F32, name=f"lower{d}")
            nc.vector.tensor_tensor(lower[:], neighbour, running[d % 2][:], MIN)
            running[d % 2] = lower
        x = held.tile([P, V], BF16)
        nc.vector.tensor_tensor(x[:], running[0][:], running[1][:], MIN)

        out_rows = out.rearrange("(p b) j -> p b j", b=BLOCKS)
        weight_columns = weights[:].rearrange("k (p b) -> k b p", b=BLOCKS)
        staged = held.tile([P, BLOCKS, V], F32)
        for half in range(2):
            product = psum.tile([P, HALF, V], F32, name=f"product{half}")
            for b in range(HALF):
                block = half * HALF + b
                nc.tensor.matmul(product[:, b, :], weight_columns[:, block, :], x[:], start=True, stop=True)
            staged_half = staged[:, half * HALF : (half + 1) * HALF, :]
            if half == 0:
                nc.vector.tensor_copy(staged_half, product[:])
            else:
                nc.scalar.copy(staged_half, product[:])
        nc.sync.dma_start(out_rows, staged[:])
